import numpy as np
import ml_dtypes


def mxq(x, axis, fmt="e4m3"):
    dtype, down = {"e4m3": (ml_dtypes.float8_e4m3fn, 7), "e5m2": (ml_dtypes.float8_e5m2, 14)}[fmt]
    v = np.moveaxis(np.asarray(x, np.float32).astype(ml_dtypes.bfloat16).astype(np.float64), axis, -1)
    blocks = v.reshape(v.shape[:-1] + (-1, 32))
    amax = np.abs(blocks).max(-1, keepdims=True)
    byte = np.maximum(np.where(amax > 0, np.frexp(amax)[1] - 1 + 127, 0) - down, 1)
    scale = np.exp2(byte - 127.0)
    codes = (blocks / scale).astype(np.float32).astype(dtype).astype(np.float64)
    return np.moveaxis((codes * scale).reshape(v.shape), -1, axis)


WIDE = False


def mx_kscale(k):
    if not WIDE:
        return np.ones(k)
    levels = np.array([10, -10, 5, -5, 0])
    if k % 512:
        return np.exp2(np.random.permutation(np.resize(levels, k // 32))).repeat(32)
    a = np.empty((k // 512, 16))
    for p in range(k // 512):
        a[p, :8] = np.random.permutation(np.resize(levels, 8))
        for g in range(8):
            far = levels[np.abs(levels - a[p, g]) >= 10]
            a[p, g + 8] = far[np.random.randint(len(far))]
    return np.exp2(a.ravel()).repeat(32)


def f64(x):
    return np.asarray(x).astype(np.float64)


def striped(idx):
    return np.tile(idx.reshape(-1, 16).T, (8, 1)).astype(np.uint16)


def unstriped(offs):
    return offs[:16].T.reshape(-1).astype(np.int64)


def striped8(idx):
    return np.concatenate([x.reshape(-1, 16).T for x in idx]).astype(np.uint16)


def runs(offs, k):
    lists = np.stack([offs[16 * r : 16 * r + 16].T.reshape(-1) for r in range(8)]).astype(np.int64)
    return lists[np.arange(k) % 512 // 64]


def pack_weight(w):
    k, n = w.shape
    w = f64(np.asarray(w, np.float32).astype(ml_dtypes.bfloat16)).reshape(k // 32, 32, n)
    amax = np.abs(w).max(1)
    byte = np.clip(np.where(amax > 0, np.frexp(amax)[1] - 1 + 127 - 7, 1), 1, 254)
    scaled = (w * np.exp2(127.0 - byte)[:, None, :]).reshape(k, n).astype(np.float32)
    words = np.ascontiguousarray(scaled.reshape(k // 512, 128, 4, n).transpose(0, 1, 3, 2)).astype(ml_dtypes.float8_e4m3fn).view(np.uint8)
    return words, np.ascontiguousarray(byte.astype(np.uint8).reshape(k // 512, 16, n))


def unpack_weight(words, scales):
    g, p, n, _ = words.shape
    vals = np.ascontiguousarray(words).view(ml_dtypes.float8_e4m3fn).astype(np.float64) * np.repeat(np.exp2(scales.astype(np.float64) - 127.0), 8, axis=1)[..., None]
    return vals.transpose(0, 1, 3, 2).reshape(g * 512, n)


def sigmoid(v):
    return 1.0 / (1.0 + np.exp(-np.maximum(v, -700.0)))


K, T, S, N, G, H, W = 512, 1024, 256, 512, 2048, 512, 128


def setup_inputs():
    n = np.random.standard_normal
    s = mx_kscale(K)[:, None]
    u = mx_kscale(K)
    packed_xT = pack_weight(n((K, T)) * s)
    packed_dT = pack_weight(n((K, G)) / s)
    perm = np.random.permutation(S)
    return {
        "x_words": packed_xT[0],
        "x_scales": packed_xT[1],
        "d_words": packed_dT[0],
        "d_scales": packed_dT[1],
        "gn": (np.random.uniform(0.5, 1.5, (H, 1)) * u[:, None]).astype(np.float32),
        "w1": (n((H, N)) / np.sqrt(H) / u[:, None]).astype(np.float32),
        "sl": np.random.uniform(1.0, 2.0, (N, 1)).astype(np.float32),
        "th": (0.5 * n((N, 1))).astype(np.float32),
        "offs": striped(np.random.permutation(T)[:S]),
        "k1": striped8(np.random.randint(0, G, (8, H))),
        "two": striped(np.random.permutation(T)[:S]),
        "k2": striped8(np.random.randint(0, G, (8, H))),
        "n1": striped(perm[:W]),
        "n2": striped(perm[W:]),
        "n3": striped(np.random.permutation(S)),
        "n4": striped(np.random.permutation(S)),
        "n5": striped(np.random.permutation(S)),
        "n6": striped(np.random.permutation(S)),
    }


def reference(x_words, x_scales, d_words, d_scales, gn, w1, sl, th, offs, k1, two, k2, n1, n2, n3, n4, n5, n6):
    d_k1 = unpack_weight(d_words, d_scales)[np.arange(K)[:, None], runs(k1, K)]
    xq = unpack_weight(x_words, x_scales)[:, unstriped(offs)]
    d_k2 = unpack_weight(d_words, d_scales)[np.arange(K)[:, None], runs(k2, K)]
    x_two = unpack_weight(x_words, x_scales)[:, unstriped(two)]
    h = 0.0625 * (d_k1.T @ xq + d_k2.T @ x_two)
    pa = h[:, unstriped(n1)]
    pb = h[:, unstriped(n2)]
    rb = pa - pb
    ua = np.zeros((H, S))
    ua[:, unstriped(n1)] = pb
    ub = ua.copy()
    ub[:, unstriped(n2)] = rb
    z = f64(gn) * (np.maximum(ub, 0.5 * ub[:, unstriped(n3)]))
    h2 = mxq(f64(w1), 0, "e4m3").T @ mxq(z, 0, "e4m3")
    ds2 = np.zeros((N, S))
    ds2[:, unstriped(n5)] = h2
    ds = np.zeros((N, S))
    ds[:, unstriped(n4)] = h2
    sg = sigmoid(f64(sl) * (ds[:, unstriped(n6)] - f64(th)))
    return ds2 * sg

@@ -1,0 +1,259 @@
+from contextlib import ExitStack
+
+import concourse.mybir as mybir
+
+K, T, S, N, G, H, W = 512, 1024, 256, 512, 2048, 512, 128
+FLOPS = 2 * (2 * K * H * S + H * N * S)
+
+F32 = mybir.dt.float32
+BF16 = mybir.dt.bfloat16
+I32 = mybir.dt.int32
+U32 = mybir.dt.uint32
+U16 = mybir.dt.uint16
+U8 = mybir.dt.uint8
+FP8X4 = mybir.dt.float8_e4m3fn_x4
+ALU = mybir.AluOpType
+ACT = mybir.ActivationFunctionType
+
+P = 128
+PACK = 4
+LEAD = 64
+EARLY, LATE = (0, LEAD), (LEAD, S)
+
+
+def tile_picked_mttznswapdesntw_none_p_kernel(
+    tc, x_words, x_scales, d_words, d_scales, gn, w1, sl, th, offs, k1, two, k2, n1, n2, n3, n4, n5, n6, out
+):
+    nc = tc.nc
+    with ExitStack() as ctx:
+        held = ctx.enter_context(tc.tile_pool(name="held", bufs=1))
+        psum = ctx.enter_context(tc.psum_pool(name="psum", bufs=1))
+
+        def load_list(name, src):
+            lst = held.tile(list(src.shape), U16, name=name)
+            nc.sync.dma_start(lst[:], src)
+            return lst
+
+        def entries(lst, cols):
+            return lst[:, cols[0] // 16 : cols[1] // 16]
+
+        d_byte_table = held.tile([P, G], U8, name="d_byte_table", tag="d_bytes_then_w1")
+        x_byte_table = held.tile([P, T], U8, name="x_byte_table")
+        picked_bytes = held.tile([P, 2 * H + 2 * S], U8, name="picked_bytes", tag="picked_then_codes", align_bytes=64)
+        placed_bytes = held.tile([P, 2 * H + 2 * S], U8, name="placed_bytes", align_bytes=64)
+        nc.vector.memset(d_byte_table[:].bitcast(I32), 0)
+        nc.gpsimd.memset(x_byte_table[:].bitcast(I32), 0)
+        nc.vector.memset(placed_bytes[:].bitcast(I32), 0)
+
+        k1_t = load_list("k1_t", k1)
+        k2_t = load_list("k2_t", k2)
+        offs_t = load_list("offs_t", offs)
+        two_t = load_list("two_t", two)
+        nc.sync.dma_start(x_byte_table[0:P:8, :].bitcast(I32), x_scales[0].bitcast(I32))
+        nc.sync.dma_start(d_byte_table[0:P:8, :].bitcast(I32), d_scales[0].bitcast(I32))
+        n2_t = load_list("n2_t", n2)
+        x_word_table = held.tile([P, T], I32, name="x_word_table", tag="x_words_then_codes", align_bytes=64)
+        d_word_table = held.tile([P, G], I32, name="d_word_table")
+        nc.sync.dma_start(d_word_table[:], d_words[0].rearrange("p c r -> p (c r)").bitcast(I32))
+        nc.sync.dma_start(x_word_table[:], x_words[0].rearrange("p c r -> p (c r)").bitcast(I32))
+        n1_t = load_list("n1_t", n1)
+        n3_t = load_list("n3_t", n3)
+        gn_t = held.tile([P, PACK], F32, name="gn_t")
+        sl_t = held.tile([P, PACK], F32, name="sl_t")
+        th_t = held.tile([P, PACK], F32, name="th_t")
+        nc.sync.dma_start(gn_t[:], gn.rearrange("(p t) o -> p (t o)", t=PACK))
+        n4_t = load_list("n4_t", n4)
+        n5_t = load_list("n5_t", n5)
+        n6_t = load_list("n6_t", n6)
+        nc.sync.dma_start(sl_t[:], sl.rearrange("(p t) o -> p (t o)", t=PACK))
+        nc.sync.dma_start(th_t[:], th.rearrange("(p t) o -> p (t o)", t=PACK))
+
+        nc.vector.tensor_copy(picked_bytes[:, 2 * H : 2 * H + S], x_byte_table[:].indirect(offs_t[:]))
+        nc.vector.tensor_copy(picked_bytes[:, 2 * H + S :], x_byte_table[:].indirect(two_t[:]))
+        nc.vector.tensor_copy(picked_bytes[:, 0:H], d_byte_table[:].indirect(k1_t[:]))
+        nc.vector.tensor_copy(picked_bytes[:, H : 2 * H], d_byte_table[:].indirect(k2_t[:]))
+        for r in range(4):
+            nc.sync.dma_start(placed_bytes[r:P:32, :].bitcast(I32), picked_bytes[8 * r : P : 32, :].bitcast(I32))
+        w_raw = held.tile([P, PACK, N], F32, name="w_raw", tag="d_bytes_then_w1")
+        nc.sync.dma_start(w_raw[:], w1.rearrange("(p j) n -> p j n", j=PACK))
+
+        x_codes = [
+            held.tile([P, S], U32, name="x_codes0", align_bytes=64),
+            held.tile([P, S], U32, name="x_codes1", tag="picked_then_codes", align_bytes=64),
+        ]
+        d_picked = held.tile([P, 2, H], U32, name="d_picked", align_bytes=64)
+        d_codes = [held.tile([P, 2, P], U32, name="d_codes0", align_bytes=64)[:]]
+        d_bytes = [held.tile([P, 2, P], U8, name=f"d_bytes{t}", align_bytes=64) for t in range(PACK)]
+
+        def deal_codes(t):
+            nc.vector.tensor_copy(d_codes[t], d_picked[:].rearrange("p l (m t) -> p t l m", t=PACK)[:, t])
+
+        def deal_bytes(t):
+            nc.vector.tensor_copy(
+                d_bytes[t][:], placed_bytes[:, 0 : 2 * H].rearrange("p (l m t) -> p t l m", l=2, t=PACK)[:, t]
+            )
+
+        nc.vector.tensor_copy(d_picked[:, 0, :], d_word_table[:].bitcast(U32).indirect(k1_t[:]))
+        nc.vector.tensor_copy(d_picked[:, 1, :], d_word_table[:].bitcast(U32).indirect(k2_t[:]))
+        deal_codes(0)
+        nc.vector.tensor_copy(x_codes[0][:], x_word_table[:].bitcast(U32).indirect(offs_t[:]))
+        deal_bytes(0)
+        nc.vector.tensor_copy(x_codes[1][:], x_word_table[:].bitcast(U32).indirect(two_t[:]))
+
+        d_codes_later = held.tile([P, PACK - 1, 2, P], U32, name="d_codes_later", tag="x_words_then_codes", align_bytes=64)
+        d_codes.extend(d_codes_later[:, t] for t in range(PACK - 1))
+
+        h = [held.tile([P, S], F32, name=f"h{t}") for t in range(PACK)]
+
+        def first_product(t):
+            if t > 0:
+                deal_codes(t)
+                deal_bytes(t)
+            acc = psum.tile([P, S], F32, name=f"h_acc{t}", tag=f"wide{t}")
+            for l in range(2):
+                nc.tensor.matmul_mx(
+                    out=acc[:],
+                    lhsT=d_codes[t][:, l, :].bitcast(FP8X4),
+                    lhsT_scale=d_bytes[t][:, l, :],
+                    rhs=x_codes[l][:].bitcast(FP8X4),
+                    rhs_scale=placed_bytes[:, 2 * H + l * S : 2 * H + (l + 1) * S],
+                    start=(l == 0),
+                    stop=(l == 1),
+                )
+            if t == 0:
+                nc.scalar.activation(h[t][:], acc[:], ACT.Copy, scale=0.0625)
+            else:
+                nc.vector.tensor_scalar(h[t][:], acc[:], 0.0625, None, ALU.mult)
+
+        w_codes = held.tile([P, N], U32, name="w_codes", align_bytes=64)
+        w_bytes = held.tile([P, N], U8, name="w_bytes", align_bytes=64)
+        w_grouped = held.tile([P, PACK, P, PACK], BF16, name="w_grouped", tag="w_then_z", align_bytes=64)
+
+        def cast_w(t):
+            nc.vector.tensor_copy(w_grouped[:, t], w_raw[:].rearrange("p j (m t) -> p t m j", t=PACK)[:, t])
+
+        def quantise_w(t):
+            nc.vector.quantize_mx(
+                out=w_codes[:, t * P : (t + 1) * P].bitcast(FP8X4),
+                scales=w_bytes[:, t * P : (t + 1) * P],
+                in_=w_grouped[:, t].rearrange("p m j -> p (m j)"),
+            )
+
+        pa = [held.tile([P, W], F32, name=f"pa{t}") for t in range(PACK)]
+        pb = [held.tile([P, W], F32, name=f"pb{t}") for t in range(PACK)]
+        rb = [held.tile([P, W], F32, name=f"rb{t}") for t in range(PACK)]
+        ub = [held.tile([P, S], F32, name=f"ub{t}") for t in range(PACK)]
+
+        def fetch_pb(t):
+            nc.scalar.activation(pb[t][:], h[t][:].indirect(n2_t[:]), ACT.Copy)
+
+        def fetch_pa(t):
+            nc.scalar.activation(pa[t][:], h[t][:].indirect(n1_t[:]), ACT.Copy)
+            nc.vector.tensor_tensor(rb[t][:], pa[t][:], pb[t][:], ALU.subtract)
+
+        def put_pb(t):
+            nc.scalar.activation(ub[t][:].indirect(n1_t[:]), pb[t][:], ACT.Copy)
+
+        def put_rb(t):
+            nc.scalar.activation(ub[t][:].indirect(n2_t[:]), rb[t][:], ACT.Copy)
+
+        first_product(0)
+        fetch_pb(0)
+        fetch_pa(0)
+        for t in range(PACK - 1):
+            first_product(t + 1)
+            put_pb(t)
+            fetch_pb(t + 1)
+            put_rb(t)
+            fetch_pa(t + 1)
+        for t in range(PACK):
+            cast_w(t)
+        for t in range(PACK):
+            quantise_w(t)
+        bias = held.tile([P, PACK], F32, name="bias")
+        nc.vector.scalar_tensor_tensor(bias[:], sl_t[:], -1.0, th_t[:], ALU.mult, ALU.mult)
+        z_early = held.tile([P, LEAD, PACK], BF16, name="z_early", tag="w_then_z", align_bytes=64)
+
+        def larger_of(t, cols, far, larger):
+            nc.scalar.activation(far, ub[t][:].indirect(entries(n3_t, cols)), ACT.Copy)
+            nc.vector.scalar_tensor_tensor(larger, far, 0.5, ub[t][:, cols[0] : cols[1]], ALU.mult, ALU.max)
+
+        def make_z_early(t):
+            far = held.tile([P, LEAD], F32, name=f"far_early{t}")
+            larger = held.tile([P, LEAD], F32, name=f"larger_early{t}")
+            larger_of(t, EARLY, far[:], larger[:])
+            nc.vector.tensor_scalar(z_early[:, :, t], larger[:], gn_t[:, t : t + 1], None, ALU.mult)
+
+        put_pb(3)
+        make_z_early(0)
+        make_z_early(1)
+        put_rb(3)
+        make_z_early(2)
+        make_z_early(3)
+
+        h2 = [held.tile([P, S], F32, name=f"h2_{t}") for t in range(PACK)]
+        z_codes = held.tile([P, S], U32, name="z_codes", align_bytes=64)
+        z_bytes = held.tile([P, S], U8, name="z_bytes", align_bytes=64)
+
+        def second_product(z, pieces, bank):
+            first, last = pieces[0][0], pieces[-1][1]
+            for lo, hi in pieces:
+                nc.vector.quantize_mx(
+                    out=z_codes[:, lo:hi].bitcast(FP8X4),
+                    scales=z_bytes[:, lo:hi],
+                    in_=z[:, lo - first : hi - first, :].rearrange("p n t -> p (n t)"),
+                )
+            for t in range(PACK):
+                acc = psum.tile([P, S], F32, name=f"h2_acc{t}", tag=f"{bank}{t}")
+                for lo, hi in pieces:
+                    nc.tensor.matmul_mx(
+                        out=acc[:, lo:hi],
+                        lhsT=w_codes[:, t * P : (t + 1) * P].bitcast(FP8X4),
+                        lhsT_scale=w_bytes[:, t * P : (t + 1) * P],
+                        rhs=z_codes[:, lo:hi].bitcast(FP8X4),
+                        rhs_scale=z_bytes[:, lo:hi],
+                        start=True,
+                        stop=True,
+                    )
+                nc.vector.tensor_copy(h2[t][:, first:last], acc[:, first:last])
+
+        second_product(z_early, [EARLY], "narrow")
+
+        far_late = held.tile([P, PACK, S - LEAD], F32, name="far_late", tag="rb3")
+        larger_late = held.tile([P, PACK, S - LEAD], F32, name="larger_late", tag="w_then_z", align_bytes=64)
+        z_late = held.tile([P, S - LEAD, PACK], BF16, name="z_late", align_bytes=64)
+        gained_late = held.tile([P, PACK, S - LEAD], F32, name="gained_late")
+        for t in range(PACK):
+            larger_of(t, LATE, far_late[:, t, :], larger_late[:, t, :])
+            nc.vector.tensor_scalar(gained_late[:, t, :], larger_late[:, t, :], gn_t[:, t : t + 1], None, ALU.mult)
+        nc.vector.tensor_copy(z_late[:], gained_late[:].rearrange("p t n -> p n t"))
+        second_product(z_late, [(LEAD, 2 * LEAD), (2 * LEAD, S)], "wide")
+
+        ds = [held.tile([P, S], F32, name=f"ds{t}") for t in range(PACK)]
+        ds2 = [held.tile([P, S], F32, name=f"ds2_{t}") for t in range(PACK)]
+        out_rows = out.rearrange("(p t) j -> p t j", t=PACK)
+
+        def send(t, cols):
+            lo, hi = cols
+            nc.scalar.activation(ds[t][:].indirect(entries(n4_t, cols)), h2[t][:, lo:hi], ACT.Copy)
+            nc.scalar.activation(ds2[t][:].indirect(entries(n5_t, cols)), h2[t][:, lo:hi], ACT.Copy)
+
+        for t in range(PACK):
+            send(t, EARLY)
+        for t in range(PACK):
+            send(t, LATE)
+            sg = held.tile([P, S], F32, name=f"sg{t}")
+            res = held.tile([P, S], F32, name=f"res{t}")
+            halves = ((0, W), (W, S))
+            stores = halves if t == PACK - 1 else ((0, S),)
+            for lo, hi in halves:
+                nc.scalar.activation(
+                    sg[:, lo:hi],
+                    ds[t][:].indirect(entries(n6_t, (lo, hi))),
+                    ACT.Sigmoid,
+                    bias=bias[:, t : t + 1],
+                    scale=sl_t[:, t : t + 1],
+                )
+            for lo, hi in stores:
+                nc.vector.tensor_tensor(res[:, lo:hi], ds2[t][:, lo:hi], sg[:, lo:hi], ALU.mult)
+                nc.sync.dma_start(out_rows[:, t, lo:hi], res[:, lo:hi])

@@ -68,6 +68,11 @@ def tile_picked_mttznswapdesntw_none_p_kernel(
         nc.sync.dma_start(sl_t[:], sl.rearrange("(p t) o -> p (t o)", t=PACK))
         nc.sync.dma_start(th_t[:], th.rearrange("(p t) o -> p (t o)", t=PACK))
 
+        warm_in = held.tile([P, 1], F32, name="warm_in")
+        warm_out = held.tile([P, 1], F32, name="warm_out")
+        nc.vector.memset(warm_in[:], 0.0)
+        nc.scalar.activation(warm_out[:], warm_in[:], ACT.Sigmoid)
+
         nc.vector.tensor_copy(picked_bytes[:, 2 * H : 2 * H + S], x_byte_table[:].indirect(offs_t[:]))
         nc.vector.tensor_copy(picked_bytes[:, 2 * H + S :], x_byte_table[:].indirect(two_t[:]))
         nc.vector.tensor_copy(picked_bytes[:, 0:H], d_byte_table[:].indirect(k1_t[:]))

@@ -132,7 +132,6 @@ def tile_picked_mttznswapdesntw_none_p_kernel(
 
         w_codes = held.tile([P, N], U32, name="w_codes", align_bytes=64)
         w_bytes = held.tile([P, N], U8, name="w_bytes", align_bytes=64)
-        w_grouped = held.tile([P, PACK, P, PACK], BF16, name="w_grouped", tag="w_then_z", align_bytes=64)
 
         def cast_w(t):
             nc.vector.tensor_copy(w_grouped[:, t], w_raw[:].rearrange("p j (m t) -> p t m j", t=PACK)[:, t])
@@ -146,7 +145,7 @@ def tile_picked_mttznswapdesntw_none_p_kernel(
 
         pa = [held.tile([P, W], F32, name=f"pa{t}") for t in range(PACK)]
         pb = [held.tile([P, W], F32, name=f"pb{t}") for t in range(PACK)]
-        rb = [held.tile([P, W], F32, name=f"rb{t}") for t in range(PACK)]
+        rb = [held.tile([P, W], F32, name=f"rb{t}") for t in range(2)]
         ub = [held.tile([P, S], F32, name=f"ub{t}") for t in range(PACK)]
 
         def fetch_pb(t):
@@ -165,36 +164,47 @@ def tile_picked_mttznswapdesntw_none_p_kernel(
         first_product(0)
         fetch_pb(0)
         fetch_pa(0)
-        for t in range(PACK - 1):
-            first_product(t + 1)
-            put_pb(t)
-            fetch_pb(t + 1)
-            put_rb(t)
-            fetch_pa(t + 1)
+        for t in range(1, PACK):
+            first_product(t)
+        put_pb(0)
+        fetch_pb(1)
+        fetch_pa(1)
+        w_grouped = held.tile([P, PACK, P, PACK], BF16, name="w_grouped", tag="x_words_then_codes", align_bytes=64)
         for t in range(PACK):
             cast_w(t)
+        rb.append(held.tile([P, W], F32, name="rb2", tag="d_bytes_then_w1"))
+        put_rb(0)
+        put_pb(1)
+        fetch_pb(2)
+        fetch_pa(2)
         for t in range(PACK):
             quantise_w(t)
+        rb.append(held.tile([P, W], F32, name="rb3", tag="x_words_then_codes", align_bytes=64))
+        put_rb(1)
+        put_pb(2)
+        fetch_pb(3)
+        fetch_pa(3)
         bias = held.tile([P, PACK], F32, name="bias")
         nc.vector.scalar_tensor_tensor(bias[:], sl_t[:], -1.0, th_t[:], ALU.mult, ALU.mult)
-        z_early = held.tile([P, LEAD, PACK], BF16, name="z_early", tag="w_then_z", align_bytes=64)
+        z_early = held.tile([P, LEAD, PACK], BF16, name="z_early", tag="z_early", align_bytes=64)
 
         def larger_of(t, cols, far, larger):
             nc.scalar.activation(far, ub[t][:].indirect(entries(n3_t, cols)), ACT.Copy)
             nc.vector.scalar_tensor_tensor(larger, far, 0.5, ub[t][:, cols[0] : cols[1]], ALU.mult, ALU.max)
 
-        def make_z_early(t):
-            far = held.tile([P, LEAD], F32, name=f"far_early{t}")
+        def make_z_early(t, buffer):
+            far = held.tile([P, LEAD], F32, name=f"far_early{t}", tag=buffer)
             larger = held.tile([P, LEAD], F32, name=f"larger_early{t}")
             larger_of(t, EARLY, far[:], larger[:])
             nc.vector.tensor_scalar(z_early[:, :, t], larger[:], gn_t[:, t : t + 1], None, ALU.mult)
 
         put_pb(3)
-        make_z_early(0)
-        make_z_early(1)
+        put_rb(2)
+        make_z_early(0, "far_early0")
         put_rb(3)
-        make_z_early(2)
-        make_z_early(3)
+        make_z_early(1, "pb3")
+        make_z_early(2, "pa3")
+        make_z_early(3, "far_early3")
 
         h2 = [held.tile([P, S], F32, name=f"h2_{t}") for t in range(PACK)]
         z_codes = held.tile([P, S], U32, name="z_codes", align_bytes=64)
@@ -224,8 +234,8 @@ def tile_picked_mttznswapdesntw_none_p_kernel(
 
         second_product(z_early, [EARLY], "narrow")
 
-        far_late = held.tile([P, PACK, S - LEAD], F32, name="far_late", tag="rb3")
-        larger_late = held.tile([P, PACK, S - LEAD], F32, name="larger_late", tag="w_then_z", align_bytes=64)
+        far_late = held.tile([P, PACK, S - LEAD], F32, name="far_late", tag="x_words_then_codes", align_bytes=64)
+        larger_late = held.tile([P, PACK, S - LEAD], F32, name="larger_late", tag="z_early", align_bytes=64)
         z_late = held.tile([P, S - LEAD, PACK], BF16, name="z_late", align_bytes=64)
         gained_late = held.tile([P, PACK, S - LEAD], F32, name="gained_late")
         for t in range(PACK):

from contextlib import ExitStack

import concourse.mybir as mybir

K, T, S, N, G, H, W = 512, 1024, 256, 512, 2048, 512, 128
FLOPS = 2 * (2 * K * H * S + H * N * S)

F32 = mybir.dt.float32
BF16 = mybir.dt.bfloat16
I32 = mybir.dt.int32
U32 = mybir.dt.uint32
U16 = mybir.dt.uint16
U8 = mybir.dt.uint8
FP8X4 = mybir.dt.float8_e4m3fn_x4
ALU = mybir.AluOpType
ACT = mybir.ActivationFunctionType

P = 128
PACK = 4
LEAD = 64
EARLY, LATE = (0, LEAD), (LEAD, S)


def tile_picked_mttznswapdesntw_none_p_kernel(
    tc, x_words, x_scales, d_words, d_scales, gn, w1, sl, th, offs, k1, two, k2, n1, n2, n3, n4, n5, n6, out
):
    nc = tc.nc
    with ExitStack() as ctx:
        held = ctx.enter_context(tc.tile_pool(name="held", bufs=1))
        psum = ctx.enter_context(tc.psum_pool(name="psum", bufs=1))

        def load_list(name, src):
            lst = held.tile(list(src.shape), U16, name=name)
            nc.sync.dma_start(lst[:], src)
            return lst

        def entries(lst, cols):
            return lst[:, cols[0] // 16 : cols[1] // 16]

        d_byte_table = held.tile([P, G], U8, name="d_byte_table", tag="d_bytes_then_w1")
        x_byte_table = held.tile([P, T], U8, name="x_byte_table")
        picked_bytes = held.tile([P, 2 * H + 2 * S], U8, name="picked_bytes", tag="picked_then_codes", align_bytes=64)
        placed_bytes = held.tile([P, 2 * H + 2 * S], U8, name="placed_bytes", align_bytes=64)
        nc.vector.memset(d_byte_table[:].bitcast(I32), 0)
        nc.gpsimd.memset(x_byte_table[:].bitcast(I32), 0)
        nc.vector.memset(placed_bytes[:].bitcast(I32), 0)

        k1_t = load_list("k1_t", k1)
        k2_t = load_list("k2_t", k2)
        offs_t = load_list("offs_t", offs)
        two_t = load_list("two_t", two)
        nc.sync.dma_start(x_byte_table[0:P:8, :].bitcast(I32), x_scales[0].bitcast(I32))
        nc.sync.dma_start(d_byte_table[0:P:8, :].bitcast(I32), d_scales[0].bitcast(I32))
        n2_t = load_list("n2_t", n2)
        x_word_table = held.tile([P, T], I32, name="x_word_table", tag="x_words_then_codes", align_bytes=64)
        d_word_table = held.tile([P, G], I32, name="d_word_table")
        nc.sync.dma_start(d_word_table[:], d_words[0].rearrange("p c r -> p (c r)").bitcast(I32))
        nc.sync.dma_start(x_word_table[:], x_words[0].rearrange("p c r -> p (c r)").bitcast(I32))
        n1_t = load_list("n1_t", n1)
        n3_t = load_list("n3_t", n3)
        gn_t = held.tile([P, PACK], F32, name="gn_t")
        sl_t = held.tile([P, PACK], F32, name="sl_t")
        th_t = held.tile([P, PACK], F32, name="th_t")
        nc.sync.dma_start(gn_t[:], gn.rearrange("(p t) o -> p (t o)", t=PACK))
        n4_t = load_list("n4_t", n4)
        n5_t = load_list("n5_t", n5)
        n6_t = load_list("n6_t", n6)
        nc.sync.dma_start(sl_t[:], sl.rearrange("(p t) o -> p (t o)", t=PACK))
        nc.sync.dma_start(th_t[:], th.rearrange("(p t) o -> p (t o)", t=PACK))

        warm_in = held.tile([P, 1], F32, name="warm_in")
        warm_out = held.tile([P, 1], F32, name="warm_out")
        nc.vector.memset(warm_in[:], 0.0)
        nc.scalar.activation(warm_out[:], warm_in[:], ACT.Sigmoid)

        nc.vector.tensor_copy(picked_bytes[:, 2 * H : 2 * H + S], x_byte_table[:].indirect(offs_t[:]))
        nc.vector.tensor_copy(picked_bytes[:, 2 * H + S :], x_byte_table[:].indirect(two_t[:]))
        nc.vector.tensor_copy(picked_bytes[:, 0:H], d_byte_table[:].indirect(k1_t[:]))
        nc.vector.tensor_copy(picked_bytes[:, H : 2 * H], d_byte_table[:].indirect(k2_t[:]))
        for r in range(4):
            nc.sync.dma_start(placed_bytes[r:P:32, :].bitcast(I32), picked_bytes[8 * r : P : 32, :].bitcast(I32))
        w_raw = held.tile([P, PACK, N], F32, name="w_raw", tag="d_bytes_then_w1")
        nc.sync.dma_start(w_raw[:], w1.rearrange("(p j) n -> p j n", j=PACK))

        x_codes = [
            held.tile([P, S], U32, name="x_codes0", align_bytes=64),
            held.tile([P, S], U32, name="x_codes1", tag="picked_then_codes", align_bytes=64),
        ]
        d_picked = held.tile([P, 2, H], U32, name="d_picked", align_bytes=64)
        d_codes = [held.tile([P, 2, P], U32, name="d_codes0", align_bytes=64)[:]]
        d_bytes = [held.tile([P, 2, P], U8, name=f"d_bytes{t}", align_bytes=64) for t in range(PACK)]

        def deal_codes(t):
            nc.vector.tensor_copy(d_codes[t], d_picked[:].rearrange("p l (m t) -> p t l m", t=PACK)[:, t])

        def deal_bytes(t):
            nc.vector.tensor_copy(
                d_bytes[t][:], placed_bytes[:, 0 : 2 * H].rearrange("p (l m t) -> p t l m", l=2, t=PACK)[:, t]
            )

        nc.vector.tensor_copy(d_picked[:, 0, :], d_word_table[:].bitcast(U32).indirect(k1_t[:]))
        nc.vector.tensor_copy(d_picked[:, 1, :], d_word_table[:].bitcast(U32).indirect(k2_t[:]))
        deal_codes(0)
        nc.vector.tensor_copy(x_codes[0][:], x_word_table[:].bitcast(U32).indirect(offs_t[:]))
        deal_bytes(0)
        nc.vector.tensor_copy(x_codes[1][:], x_word_table[:].bitcast(U32).indirect(two_t[:]))

        d_codes_later = held.tile([P, PACK - 1, 2, P], U32, name="d_codes_later", tag="x_words_then_codes", align_bytes=64)
        d_codes.extend(d_codes_later[:, t] for t in range(PACK - 1))

        h = [held.tile([P, S], F32, name=f"h{t}") for t in range(PACK)]

        def first_product(t):
            if t > 0:
                deal_codes(t)
                deal_bytes(t)
            acc = psum.tile([P, S], F32, name=f"h_acc{t}", tag=f"wide{t}")
            for l in range(2):
                nc.tensor.matmul_mx(
                    out=acc[:],
                    lhsT=d_codes[t][:, l, :].bitcast(FP8X4),
                    lhsT_scale=d_bytes[t][:, l, :],
                    rhs=x_codes[l][:].bitcast(FP8X4),
                    rhs_scale=placed_bytes[:, 2 * H + l * S : 2 * H + (l + 1) * S],
                    start=(l == 0),
                    stop=(l == 1),
                )
            if t == 0:
                nc.scalar.activation(h[t][:], acc[:], ACT.Copy, scale=0.0625)
            else:
                nc.vector.tensor_scalar(h[t][:], acc[:], 0.0625, None, ALU.mult)

        w_codes = held.tile([P, N], U32, name="w_codes", align_bytes=64)
        w_bytes = held.tile([P, N], U8, name="w_bytes", align_bytes=64)

        def cast_w(t):
            nc.vector.tensor_copy(w_grouped[:, t], w_raw[:].rearrange("p j (m t) -> p t m j", t=PACK)[:, t])

        def quantise_w(t):
            nc.vector.quantize_mx(
                out=w_codes[:, t * P : (t + 1) * P].bitcast(FP8X4),
                scales=w_bytes[:, t * P : (t + 1) * P],
                in_=w_grouped[:, t].rearrange("p m j -> p (m j)"),
            )

        pa = [held.tile([P, W], F32, name=f"pa{t}") for t in range(PACK)]
        pb = [held.tile([P, W], F32, name=f"pb{t}") for t in range(PACK)]
        rb = [held.tile([P, W], F32, name=f"rb{t}") for t in range(2)]
        ub = [held.tile([P, S], F32, name=f"ub{t}") for t in range(PACK)]

        def fetch_pb(t):
            nc.scalar.activation(pb[t][:], h[t][:].indirect(n2_t[:]), ACT.Copy)

        def fetch_pa(t):
            nc.scalar.activation(pa[t][:], h[t][:].indirect(n1_t[:]), ACT.Copy)
            nc.vector.tensor_tensor(rb[t][:], pa[t][:], pb[t][:], ALU.subtract)

        def put_pb(t):
            nc.scalar.activation(ub[t][:].indirect(n1_t[:]), pb[t][:], ACT.Copy)

        def put_rb(t):
            nc.scalar.activation(ub[t][:].indirect(n2_t[:]), rb[t][:], ACT.Copy)

        first_product(0)
        fetch_pb(0)
        fetch_pa(0)
        for t in range(1, PACK):
            first_product(t)
        put_pb(0)
        fetch_pb(1)
        fetch_pa(1)
        w_grouped = held.tile([P, PACK, P, PACK], BF16, name="w_grouped", tag="x_words_then_codes", align_bytes=64)
        for t in range(PACK):
            cast_w(t)
        rb.append(held.tile([P, W], F32, name="rb2", tag="d_bytes_then_w1"))
        put_rb(0)
        put_pb(1)
        fetch_pb(2)
        fetch_pa(2)
        for t in range(PACK):
            quantise_w(t)
        rb.append(held.tile([P, W], F32, name="rb3", tag="x_words_then_codes", align_bytes=64))
        put_rb(1)
        put_pb(2)
        fetch_pb(3)
        fetch_pa(3)
        bias = held.tile([P, PACK], F32, name="bias")
        nc.vector.scalar_tensor_tensor(bias[:], sl_t[:], -1.0, th_t[:], ALU.mult, ALU.mult)
        z_early = held.tile([P, LEAD, PACK], BF16, name="z_early", tag="z_early", align_bytes=64)

        def larger_of(t, cols, far, larger):
            nc.scalar.activation(far, ub[t][:].indirect(entries(n3_t, cols)), ACT.Copy)
            nc.vector.scalar_tensor_tensor(larger, far, 0.5, ub[t][:, cols[0] : cols[1]], ALU.mult, ALU.max)

        def make_z_early(t, buffer):
            far = held.tile([P, LEAD], F32, name=f"far_early{t}", tag=buffer)
            larger = held.tile([P, LEAD], F32, name=f"larger_early{t}")
            larger_of(t, EARLY, far[:], larger[:])
            nc.vector.tensor_scalar(z_early[:, :, t], larger[:], gn_t[:, t : t + 1], None, ALU.mult)

        put_pb(3)
        put_rb(2)
        make_z_early(0, "far_early0")
        put_rb(3)
        make_z_early(1, "pb3")
        make_z_early(2, "pa3")
        make_z_early(3, "far_early3")

        h2 = [held.tile([P, S], F32, name=f"h2_{t}") for t in range(PACK)]
        z_codes = held.tile([P, S], U32, name="z_codes", align_bytes=64)
        z_bytes = held.tile([P, S], U8, name="z_bytes", align_bytes=64)

        def second_product(z, pieces, bank):
            first, last = pieces[0][0], pieces[-1][1]
            for lo, hi in pieces:
                nc.vector.quantize_mx(
                    out=z_codes[:, lo:hi].bitcast(FP8X4),
                    scales=z_bytes[:, lo:hi],
                    in_=z[:, lo - first : hi - first, :].rearrange("p n t -> p (n t)"),
                )
            for t in range(PACK):
                acc = psum.tile([P, S], F32, name=f"h2_acc{t}", tag=f"{bank}{t}")
                for lo, hi in pieces:
                    nc.tensor.matmul_mx(
                        out=acc[:, lo:hi],
                        lhsT=w_codes[:, t * P : (t + 1) * P].bitcast(FP8X4),
                        lhsT_scale=w_bytes[:, t * P : (t + 1) * P],
                        rhs=z_codes[:, lo:hi].bitcast(FP8X4),
                        rhs_scale=z_bytes[:, lo:hi],
                        start=True,
                        stop=True,
                    )
                nc.vector.tensor_copy(h2[t][:, first:last], acc[:, first:last])

        second_product(z_early, [EARLY], "narrow")

        far_late = held.tile([P, PACK, S - LEAD], F32, name="far_late", tag="x_words_then_codes", align_bytes=64)
        larger_late = held.tile([P, PACK, S - LEAD], F32, name="larger_late", tag="z_early", align_bytes=64)
        z_late = held.tile([P, S - LEAD, PACK], BF16, name="z_late", align_bytes=64)
        gained_late = held.tile([P, PACK, S - LEAD], F32, name="gained_late")
        for t in range(PACK):
            larger_of(t, LATE, far_late[:, t, :], larger_late[:, t, :])
            nc.vector.tensor_scalar(gained_late[:, t, :], larger_late[:, t, :], gn_t[:, t : t + 1], None, ALU.mult)
        nc.vector.tensor_copy(z_late[:], gained_late[:].rearrange("p t n -> p n t"))
        second_product(z_late, [(LEAD, 2 * LEAD), (2 * LEAD, S)], "wide")

        ds = [held.tile([P, S], F32, name=f"ds{t}") for t in range(PACK)]
        ds2 = [held.tile([P, S], F32, name=f"ds2_{t}") for t in range(PACK)]
        out_rows = out.rearrange("(p t) j -> p t j", t=PACK)

        def send(t, cols):
            lo, hi = cols
            nc.scalar.activation(ds[t][:].indirect(entries(n4_t, cols)), h2[t][:, lo:hi], ACT.Copy)
            nc.scalar.activation(ds2[t][:].indirect(entries(n5_t, cols)), h2[t][:, lo:hi], ACT.Copy)

        for t in range(PACK):
            send(t, EARLY)
        for t in range(PACK):
            send(t, LATE)
            sg = held.tile([P, S], F32, name=f"sg{t}")
            res = held.tile([P, S], F32, name=f"res{t}")
            halves = ((0, W), (W, S))
            stores = halves if t == PACK - 1 else ((0, S),)
            for lo, hi in halves:
                nc.scalar.activation(
                    sg[:, lo:hi],
                    ds[t][:].indirect(entries(n6_t, (lo, hi))),
                    ACT.Sigmoid,
                    bias=bias[:, t : t + 1],
                    scale=sl_t[:, t : t + 1],
                )
            for lo, hi in stores:
                nc.vector.tensor_tensor(res[:, lo:hi], ds2[t][:, lo:hi], sg[:, lo:hi], ALU.mult)
                nc.sync.dma_start(out_rows[:, t, lo:hi], res[:, lo:hi])
